import numpy as np
import ml_dtypes


def mxq(x, axis, fmt="e4m3"):
    dtype, down = {"e4m3": (ml_dtypes.float8_e4m3fn, 7), "e5m2": (ml_dtypes.float8_e5m2, 14)}[fmt]
    v = np.moveaxis(np.asarray(x, np.float32).astype(ml_dtypes.bfloat16).astype(np.float64), axis, -1)
    blocks = v.reshape(v.shape[:-1] + (-1, 32))
    amax = np.abs(blocks).max(-1, keepdims=True)
    byte = np.maximum(np.where(amax > 0, np.frexp(amax)[1] - 1 + 127, 0) - down, 1)
    scale = np.exp2(byte - 127.0)
    codes = (blocks / scale).astype(np.float32).astype(dtype).astype(np.float64)
    return np.moveaxis((codes * scale).reshape(v.shape), -1, axis)


WIDE = False


def mx_kscale(k):
    if not WIDE:
        return np.ones(k)
    levels = np.array([10, -10, 5, -5, 0])
    if k % 512:
        return np.exp2(np.random.permutation(np.resize(levels, k // 32))).repeat(32)
    a = np.empty((k // 512, 16))
    for p in range(k // 512):
        a[p, :8] = np.random.permutation(np.resize(levels, 8))
        for g in range(8):
            far = levels[np.abs(levels - a[p, g]) >= 10]
            a[p, g + 8] = far[np.random.randint(len(far))]
    return np.exp2(a.ravel()).repeat(32)


def f64(x):
    return np.asarray(x).astype(np.float64)


def striped(idx):
    return np.tile(idx.reshape(-1, 16).T, (8, 1)).astype(np.uint16)


def unstriped(offs):
    return offs[:16].T.reshape(-1).astype(np.int64)


def relu(v):
    return np.maximum(v, 0.0)


K, T, D, S, V, H, N = 512, 512, 4, 1024, 256, 512, 256


def setup_inputs():
    n = np.random.standard_normal
    s = mx_kscale(K)[:, None]
    u = mx_kscale(H)
    return {
        "xT": (n((K, T)) * s).astype(np.float32),
        "w1": (n((K, H)) / np.sqrt(K) / s * u).astype(np.float32),
        "w2": (n((H, N)) / np.sqrt(H) / u[:, None]).astype(np.float32),
        "offs": striped(np.concatenate([np.random.permutation(T)[:V] for _ in range(D)])),
    }


def reference(xT, w1, w2, offs):
    idx = unstriped(offs)
    x = np.empty((K, V))
    for l in range(D):
        r = l // 4 * (4 * K // D) + l % 4 + 4 * np.arange(K // D)
        x[r] = f64(xT)[r][:, idx[l * V:(l + 1) * V]]
    xq = mxq(x, 0, "e4m3")
    h = relu(mxq(f64(w1), 0, "e4m3").T @ xq)
    return mxq(f64(w2), 0, "e4m3").T @ mxq(h, 0, "e4m3")

from contextlib import ExitStack

import concourse.mybir as mybir

K, T, D, V, H, N = 512, 512, 4, 256, 512, 256
P = 128
FLOPS = 2 * K * H * V + 2 * H * N * V

F32 = mybir.dt.float32
BF16 = mybir.dt.bfloat16
U32 = mybir.dt.uint32
U16 = mybir.dt.uint16
U8 = mybir.dt.uint8
FP8X4 = mybir.dt.float8_e4m3fn_x4
RELU = mybir.ActivationFunctionType.Relu

CHUNKS = [(0, 128), (128, 256), (256, 384), (384, 512)]
HALF = 128


def tile_picked_grid_mlp_relu_sub_l_kernel(tc, xT, w1, w2, offs, out):
    nc = tc.nc
    with ExitStack() as ctx:
        keep = ctx.enter_context(tc.tile_pool(name="keep", bufs=1))
        psum = ctx.enter_context(tc.psum_pool(name="psum", bufs=1))

        offsets = keep.tile([P, D * V // 16], U16, name="offsets")
        nc.sync.dma_start(offsets[:], offs)
        x_rows = xT.rearrange("(p l) w -> p l w", l=4)
        tables = []
        for l in range(4):
            table = keep.tile([P, T], F32, name=f"table{l}")
            nc.sync.dma_start(table[:], x_rows[:, l, :])
            tables.append(table)
        w1_rows = w1.rearrange("(p j) i -> p j i", j=4)
        w1_raw = []
        for c, (a, b) in enumerate(CHUNKS):
            raw = keep.tile([P, 4, b - a], F32, name=f"w1_raw{c}")
            nc.sync.dma_start(raw[:], w1_rows[:, :, a:b])
            w1_raw.append(raw)
        w2_rows = w2.rearrange("(c t q) n -> t c q n", t=4, q=4)
        w2_raw = keep.tile([P, 4, N], F32, name="w2_raw", tag="w2_then_h", align_bytes=64)
        for t in range(4):
            nc.sync.dma_start(w2_raw[:, t, :], w2_rows[t])

        x_picked = keep.tile([P, 4, V], F32, name="x_picked")
        x_grouped = keep.tile([P, V, 4], BF16, name="x_grouped", align_bytes=64)
        x_codes = keep.tile([P, V], U32, name="x_codes", align_bytes=64)
        x_scales = keep.tile([P, V], U8, name="x_scales", align_bytes=64)
        w1_grouped = keep.tile([P, 4, 128, 4], BF16, name="w1_grouped", align_bytes=64)
        w1_codes = keep.tile([P, 4, 128], U32, name="w1_codes", align_bytes=64)
        w1_scales = keep.tile([P, 4, 128], U8, name="w1_scales", align_bytes=64)
        w2_grouped = keep.tile([P, N, 4], BF16, name="w2_grouped", align_bytes=64)
        w2_codes = keep.tile([P, N], U32, name="w2_codes", align_bytes=64)
        w2_scales = keep.tile([P, N], U8, name="w2_scales", align_bytes=64)

        def w1_copy(copy, c, t0, t1):
            a, b = CHUNKS[c]
            dst = w1_grouped[:, t0:t1, a // 4 : b // 4, :].rearrange("p t (c q) j -> p t c j q", q=4)
            src = w1_raw[c][:].rearrange("p j (c t q) -> p t c j q", t=4, q=4)[:, t0:t1]
            copy(out=dst, in_=src)

        cols = V // 16

        def gather(l, v0, v1):
            c0, c1 = l * cols + v0 // 16, l * cols + v1 // 16
            nc.vector.tensor_copy(x_picked[:, l, v0:v1], tables[l][:].indirect(offsets[:, c0:c1]))

        def x_copy(half):
            v = slice(half * HALF, (half + 1) * HALF)
            nc.vector.tensor_copy(
                out=x_grouped[:, v, :].rearrange("p (c i) t -> p c t i", i=4),
                in_=x_picked[:, :, v].rearrange("p t (c i) -> p c t i", i=4),
            )

        def quantize_x(half):
            v = slice(half * HALF, (half + 1) * HALF)
            nc.vector.quantize_mx(
                out=x_codes[:, v].bitcast(FP8X4),
                scales=x_scales[:, v],
                in_=x_grouped[:, v, :].rearrange("p v t -> p (v t)"),
            )

        def quantize_w1(t):
            nc.vector.quantize_mx(
                out=w1_codes[:, t, :].bitcast(FP8X4),
                scales=w1_scales[:, t, :],
                in_=w1_grouped[:, t, :, :].rearrange("p m j -> p (m j)"),
            )

        def w2_copy(copy, u):
            n = slice(u * 128, (u + 1) * 128)
            copy(
                out=w2_grouped[:, n, :].rearrange("p (c i) t -> p c t i", i=4),
                in_=w2_raw[:, :, n].rearrange("p t (c i) -> p c t i", i=4),
            )

        hidden = [psum.tile([P, 4, HALF], F32, name=f"hidden{half}") for half in range(2)]

        def mm1(t, half):
            v = slice(half * HALF, (half + 1) * HALF)
            nc.tensor.matmul_mx(
                out=hidden[half][:, t, :],
                lhsT=w1_codes[:, t, :].bitcast(FP8X4),
                lhsT_scale=w1_scales[:, t, :],
                rhs=x_codes[:, v].bitcast(FP8X4),
                rhs_scale=x_scales[:, v],
                start=True,
                stop=True,
            )

        for l in range(3):
            gather(l, 0, V)
        for half in range(2):
            gather(3, half * HALF, (half + 1) * HALF)
        for c in range(3):
            w1_copy(nc.scalar.copy, c, 0, 4)
        for half in range(2):
            x_copy(half)
        for half in range(2):
            quantize_x(half)
        w1_copy(nc.scalar.copy, 3, 0, 2)
        w1_copy(nc.scalar.copy, 3, 2, 4)
        for t in range(4):
            quantize_w1(t)
            for half in range(2):
                mm1(t, half)
        w2_copy(nc.scalar.copy, 0)
        w2_copy(nc.vector.tensor_copy, 1)
        h_codes, h_scales = [], []
        h_both = keep.tile([P, V, 4], BF16, name="h_both", tag="w2_then_h", align_bytes=64)
        h_grouped = [h_both[:, half * HALF : (half + 1) * HALF, :] for half in range(2)]
        for half in range(2):
            h_codes.append(keep.tile([P, HALF], U32, name=f"h_codes{half}", align_bytes=64))
            h_scales.append(keep.tile([P, HALF], U8, name=f"h_scales{half}", align_bytes=64))
        nc.vector.quantize_mx(
            out=w2_codes[:].bitcast(FP8X4), scales=w2_scales[:], in_=w2_grouped[:].rearrange("p n t -> p (n t)")
        )
        nc.scalar.activation(h_grouped[0], hidden[0][:].rearrange("p t v -> p v t"), RELU)
        nc.vector.tensor_scalar_max(h_grouped[1], hidden[1][:].rearrange("p t v -> p v t"), 0.0)
        out_view = out.rearrange("(u p) v -> p u v", u=2)
        for half in range(2):
            nc.vector.quantize_mx(
                out=h_codes[half][:].bitcast(FP8X4),
                scales=h_scales[half][:],
                in_=h_grouped[half].rearrange("p v t -> p (v t)"),
            )
            acc = psum.tile([P, 2, HALF], F32, name=f"acc{half}")
            for u in range(2):
                n = slice(u * 128, (u + 1) * 128)
                nc.tensor.matmul_mx(
                    out=acc[:, u, :],
                    lhsT=w2_codes[:, n].bitcast(FP8X4),
                    lhsT_scale=w2_scales[:, n],
                    rhs=h_codes[half][:].bitcast(FP8X4),
                    rhs_scale=h_scales[half][:],
                    start=True,
                    stop=True,
                )
            result = keep.tile([P, 2, HALF], F32, name=f"result{half}")
            if half == 0:
                nc.scalar.copy(result[:], acc[:])
            else:
                nc.vector.tensor_copy(result[:], acc[:])
            nc.sync.dma_start(out_view[:, :, half * HALF : (half + 1) * HALF], result[:])
